import numpy as np
import ml_dtypes


def mxq(x, axis, fmt="e4m3"):
    dtype, down = {"e4m3": (ml_dtypes.float8_e4m3fn, 7), "e5m2": (ml_dtypes.float8_e5m2, 14)}[fmt]
    v = np.moveaxis(np.asarray(x, np.float32).astype(ml_dtypes.bfloat16).astype(np.float64), axis, -1)
    blocks = v.reshape(v.shape[:-1] + (-1, 32))
    amax = np.abs(blocks).max(-1, keepdims=True)
    byte = np.maximum(np.where(amax > 0, np.frexp(amax)[1] - 1 + 127, 0) - down, 1)
    scale = np.exp2(byte - 127.0)
    codes = (blocks / scale).astype(np.float32).astype(dtype).astype(np.float64)
    return np.moveaxis((codes * scale).reshape(v.shape), -1, axis)


WIDE = False


def mx_kscale(k):
    if not WIDE:
        return np.ones(k)
    levels = np.array([10, -10, 5, -5, 0])
    if k % 512:
        return np.exp2(np.random.permutation(np.resize(levels, k // 32))).repeat(32)
    a = np.empty((k // 512, 16))
    for p in range(k // 512):
        a[p, :8] = np.random.permutation(np.resize(levels, 8))
        for g in range(8):
            far = levels[np.abs(levels - a[p, g]) >= 10]
            a[p, g + 8] = far[np.random.randint(len(far))]
    return np.exp2(a.ravel()).repeat(32)


def f64(x):
    return np.asarray(x).astype(np.float64)


def striped(idx):
    return np.tile(np.asarray(idx).reshape(-1, 16).T, (8, 1)).astype(np.uint16)


def unstriped(offs):
    return offs[:16].T.reshape(-1).astype(np.int64)


E2M1 = np.array([0.0, 0.5, 1.0, 1.5, 2.0, 3.0, 4.0, 6.0, -0.0, -0.5, -1.0, -1.5, -2.0, -3.0, -4.0, -6.0])


def pack_weight(w, fmt):
    k, n = w.shape
    w = f64(np.asarray(w, np.float32).astype(ml_dtypes.bfloat16)).reshape(k // 32, 32, n)
    amax = np.abs(w).max(1)
    if fmt == "e4m3":
        byte = np.frexp(amax)[1] - 1 + 127 - 7
    else:
        mant, ex = np.frexp(amax / 6.0)
        byte = np.where(mant > 0.5, ex, ex - 1) + 127
    byte = np.clip(np.where(amax > 0, byte, 1), 1, 254)
    scaled = (w * np.exp2(127.0 - byte)[:, None, :]).reshape(k, n).astype(np.float32)
    by_word = np.ascontiguousarray(scaled.reshape(k // 512, 128, 4, n).transpose(0, 1, 3, 2))
    if fmt == "e4m3":
        words = by_word.astype(ml_dtypes.float8_e4m3fn).view(np.uint8)
    else:
        c = by_word.astype(ml_dtypes.float4_e2m1fn).view(np.uint8) & 0xF
        words = (c[..., 0::2] | (c[..., 1::2] << 4)).reshape(k // 512, 128, 2 * n)
    return np.ascontiguousarray(words), np.ascontiguousarray(byte.astype(np.uint8).reshape(k // 512, 16, n))


def unpack_weight(words, scales, fmt):
    g, _, n = scales.shape
    words = np.ascontiguousarray(words).reshape(g, 128, n, -1)
    if fmt == "e4m3":
        vals = words.view(ml_dtypes.float8_e4m3fn).astype(np.float64)
    else:
        nib = np.empty((g, 128, n, 4), np.uint8)
        nib[..., 0::2] = words & 0xF
        nib[..., 1::2] = words >> 4
        vals = E2M1[nib]
    vals = vals * np.repeat(np.exp2(scales.astype(np.float64) - 127.0), 8, axis=1)[..., None]
    return vals.transpose(0, 1, 3, 2).reshape(g * 512, n)


D, E, T, I, Q = 512, 512, 2048, 512, 128


def setup_inputs():
    n = np.random.standard_normal
    idx = np.random.permutation(T)[:I]
    fd = mx_kscale(D)
    fe = mx_kscale(E)
    keysp = pack_weight(n((D, T)) / fd[:, None], "e4m3")
    valsp = pack_weight(n((E, T)) / fe[:, None], "e4m3")
    return {
        "query": (n((D, Q)) * 0.7 / np.sqrt(D) * fd[:, None]).astype(np.float32),
        "query2": (n((D, Q)) * 0.7 / np.sqrt(D) * fd[:, None]).astype(np.float32),
        "keys_words": keysp[0],
        "keys_scales": keysp[1],
        "sharp": (np.random.uniform(0.3, 1.2, (Q, 1))).astype(np.float32),
        "gout": (n((E, Q)) * 1 / np.sqrt(E) * fe[:, None]).astype(np.float32),
        "vals_words": valsp[0],
        "vals_scales": valsp[1],
        "old": (0.5 * n((Q, T))).astype(np.float32),
        "offs": striped(idx),
    }


def reference(query, query2, keys_words, keys_scales, sharp, gout, vals_words, vals_scales, old, offs):
    idx = unstriped(offs)
    keysu = unpack_weight(keys_words, keys_scales, "e4m3")
    valsu = unpack_weight(vals_words, vals_scales, "e4m3")
    queryq = mxq(f64(query), 0, "e4m3")
    keysidxg = keysu[:, idx]
    a = queryq.T @ keysidxg
    query2q = mxq(f64(query2), 0, "e4m3")
    b = query2q.T @ keysidxg
    dl = a - b
    p = np.exp(a * 0.5) / (np.square(dl) * f64(sharp) + 1.0)
    z = np.sum(p, axis=1, keepdims=True)
    goutq = mxq(f64(gout), 0, "e4m3")
    valsidxg = valsu[:, idx]
    c0 = goutq.T @ valsidxg
    dz = np.sum(c0 * p / np.square(z) * (-1.0), axis=1, keepdims=True)
    dp = c0 / z + dz
    ddl = dp * np.exp(a * 0.5) / np.square(np.square(dl) * f64(sharp) + 1.0) * (-1.0) * f64(sharp) * dl * 2.0
    da = dp / (np.square(dl) * f64(sharp) + 1.0) * np.exp(a * 0.5) * 0.5 + ddl
    gs = da * 512.0
    gf = np.zeros((Q, T))
    gf[:, idx] = gs
    y = f64(old) + gf
    return y

@@ -1,0 +1,217 @@
+from contextlib import ExitStack
+
+import concourse.mybir as mybir
+
+F32 = mybir.dt.float32
+BF16 = mybir.dt.bfloat16
+I32 = mybir.dt.int32
+U32 = mybir.dt.uint32
+U16 = mybir.dt.uint16
+U8 = mybir.dt.uint8
+FP8X4 = mybir.dt.float8_e4m3fn_x4
+ALU = mybir.AluOpType
+ACT = mybir.ActivationFunctionType
+
+P = 128
+PACK = 4
+K = P * PACK
+T = 2048
+SLOTS = 512
+ROWS = 128
+HALF = SLOTS // 2
+QUARTER = SLOTS // 4
+LIST_COLS = SLOTS // 16
+OUT_CHUNKS = (512, 512, 512, 512)
+
+FLOPS = 3 * 2 * K * ROWS * SLOTS
+
+
+def tile_attend_balikescores_s_kernel(
+    tc, query, query2, keys_words, keys_scales, sharp, gout, vals_words, vals_scales, old, offs, out
+):
+    nc = tc.nc
+    with ExitStack() as ctx:
+        sb = ctx.enter_context(tc.tile_pool(name="sb", bufs=1))
+        ps = ctx.enter_context(tc.psum_pool(name="ps", bufs=1))
+
+        def tile(name, shape, dtype, tag=None):
+            return sb.tile(shape, dtype, name=name, tag=tag or name, align_bytes=64)
+
+        def load_words(queue, dst, words):
+            queue.dma_start(out=dst[:].bitcast(I32), in_=words[0].rearrange("p n t -> p (n t)").bitcast(I32))
+
+        def load_scale_rows(queues, dst, scales):
+            rows = scales[0].bitcast(I32).rearrange("(quad j) c -> j quad c", j=4)
+            for j in range(4):
+                queues[j].dma_start(out=dst[:].bitcast(I32)[j:P:32, :], in_=rows[j])
+
+        def load_rows(queue, dst, src):
+            queue.dma_start(out=dst[:], in_=src.rearrange("(p t) q -> p t q", t=PACK))
+
+        def interleaved(grouped, raw):
+            return (
+                grouped[:].rearrange("p (c i) t -> p c t i", i=4),
+                raw[:].rearrange("p t (c i) -> p c t i", i=4),
+            )
+
+        def quantize(name, grouped):
+            codes = tile(name + "_codes", [P, ROWS], U32)
+            scales = tile(name + "_scales", [P, ROWS], U8)
+            nc.vector.quantize_mx(
+                out=codes[:].bitcast(FP8X4), scales=scales[:], in_=grouped[:].rearrange("p q t -> p (q t)")
+            )
+            return codes, scales
+
+        def product(dst, rows_operand, codes, scales, start, stop):
+            nc.tensor.matmul_mx(
+                out=dst,
+                lhsT=rows_operand[0][:].bitcast(FP8X4),
+                lhsT_scale=rows_operand[1][:],
+                rhs=codes.bitcast(FP8X4),
+                rhs_scale=scales,
+                start=start,
+                stop=stop,
+            )
+
+        offsets = tile("offsets", [P, LIST_COLS], U16)
+        key_pool = tile("key_pool", [P, T], U32)
+        key_scale_pool = tile("key_scale_pool", [P, T], U8)
+        val_scale_pool = tile("val_scale_pool", [P, T], U8)
+        q_raw = tile("q_raw", [P, PACK, ROWS], F32)
+        q2_raw = tile("q2_raw", [P, PACK, ROWS], F32)
+        sharp_col = tile("sharp_col", [P, 1], F32)
+        window = tile("window", [P, T], F32)
+        one = tile("one", [P, 1], F32)
+        warm = tile("warm", [P, 1], F32)
+
+        nc.vector.memset(key_scale_pool[:].bitcast(I32), 0)
+        nc.vector.memset(val_scale_pool[:].bitcast(I32), 0)
+        nc.gpsimd.memset(one[:], 1.0)
+        nc.scalar.activation(out=warm[:], in_=one[:], func=ACT.Ln, bias=one[:])
+
+        nc.sync.dma_start(offsets[:], offs)
+        load_rows(nc.scalar, q_raw, query)
+        load_rows(nc.scalar, q2_raw, query2)
+        load_words(nc.scalar, key_pool, keys_words)
+        load_scale_rows((nc.sync,) * 4, key_scale_pool, keys_scales)
+        load_scale_rows((nc.sync,) * 3 + (nc.gpsimd,), val_scale_pool, vals_scales)
+        nc.gpsimd.dma_start(out=sharp_col[:], in_=sharp)
+        nc.vector.memset(window[:], 0.0)
+
+        key_scales = tile("key_scales", [P, SLOTS], U8)
+        nc.vector.tensor_copy(key_scales[:], key_scale_pool[:].indirect(offsets[:]))
+
+        q_grouped = tile("q_grouped", [P, ROWS, PACK], BF16)
+        nq2_grouped = tile("nq2_grouped", [P, ROWS, PACK], BF16)
+        dst, src = interleaved(q_grouped, q_raw)
+        nc.scalar.activation(out=dst, in_=src, func=ACT.Copy)
+        dst, src = interleaved(nq2_grouped, q2_raw)
+        nc.scalar.activation(out=dst, in_=src, func=ACT.Copy, scale=-1.0)
+        g_raw = tile("g_raw", [P, PACK, ROWS], F32, tag="q_raw")
+        load_rows(nc.sync, g_raw, gout)
+        val_pool = tile("val_pool", [P, T], U32, tag="q2_raw")
+        load_words(nc.scalar, val_pool, vals_words)
+        q_mx = quantize("q", q_grouped)
+        val_scales = tile("val_scales", [P, SLOTS], U8)
+        nc.vector.tensor_copy(val_scales[:], val_scale_pool[:].indirect(offsets[:]))
+        nq2_mx = quantize("nq2", nq2_grouped)
+        sharp256 = tile("sharp256", [P, 1], F32)
+        nc.vector.tensor_scalar(sharp256[:], sharp_col[:], 256.0, None, ALU.mult)
+
+        key_codes = []
+        for h in range(2):
+            codes = tile("key_codes%d" % h, [P, HALF], U32)
+            nc.vector.tensor_copy(
+                codes[:], key_pool[:].indirect(offsets[:, h * LIST_COLS // 2 : (h + 1) * LIST_COLS // 2])
+            )
+            key_codes.append(codes)
+
+        old_sb = tile("old_sb", [P, T], F32, tag="key_pool")
+        nc.sync.dma_start(out=old_sb[:], in_=old)
+
+        a_ps = ps.tile([P, SLOTS], F32, name="a_ps")
+        nb_ps = ps.tile([P, QUARTER], F32, name="nb_ps")
+        d1_ps = ps.tile([P, QUARTER], F32, name="d1_ps")
+        d2_ps = ps.tile([P, HALF], F32, name="d2_ps")
+        c_ps = ps.tile([P, SLOTS], F32, name="c_ps")
+        first = slice(0, QUARTER)
+        second = slice(QUARTER, HALF)
+        lower = slice(0, HALF)
+        upper = slice(HALF, SLOTS)
+
+        product(nb_ps[:], nq2_mx, key_codes[0][:, first], key_scales[:, first], True, True)
+        product(a_ps[:, lower], q_mx, key_codes[0][:], key_scales[:, lower], True, True)
+        product(d1_ps[:], q_mx, key_codes[0][:, second], key_scales[:, second], True, False)
+        product(d1_ps[:], nq2_mx, key_codes[0][:, second], key_scales[:, second], False, True)
+        product(d2_ps[:], nq2_mx, key_codes[1][:], key_scales[:, upper], True, False)
+        product(d2_ps[:], q_mx, key_codes[1][:], key_scales[:, upper], False, True)
+
+        nb = tile("nb", [P, QUARTER], F32)
+        d0 = tile("d0", [P, QUARTER], F32)
+        sq = tile("sq", [P, SLOTS], F32)
+        logden = tile("logden", [P, SLOTS], F32)
+        nc.scalar.copy(nb[:], nb_ps[:])
+        nc.vector.tensor_tensor(d0[:], a_ps[:, first], nb[:], ALU.add)
+        product(a_ps[:, upper], q_mx, key_codes[1][:], key_scales[:, upper], True, True)
+        nc.scalar.activation(out=sq[:, second], in_=d1_ps[:], func=ACT.Square)
+        nc.scalar.activation(out=sq[:, first], in_=d0[:], func=ACT.Square)
+        nc.scalar.activation(out=logden[:, lower], in_=sq[:, lower], func=ACT.Ln, scale=sharp_col[:], bias=one[:])
+        nc.scalar.activation(out=sq[:, upper], in_=d2_ps[:], func=ACT.Square)
+        nc.scalar.activation(out=logden[:, upper], in_=sq[:, upper], func=ACT.Ln, scale=sharp_col[:], bias=one[:])
+
+        u0 = tile("u0", [P, SLOTS], F32)
+        for cols, dl in ((second, d1_ps), (first, d0), (upper, d2_ps)):
+            nc.vector.scalar_tensor_tensor(u0[:, cols], dl[:], -4.0, sq[:, cols], ALU.mult, ALU.add)
+        val_codes = tile("val_codes", [P, SLOTS], U32)
+        nc.vector.tensor_copy(val_codes[:], val_pool[:].indirect(offsets[:]))
+        logp = tile("logp", [P, SLOTS], F32)
+        nc.vector.scalar_tensor_tensor(logp[:], a_ps[:], 0.5, logden[:], ALU.mult, ALU.subtract)
+        g_grouped = tile("g_grouped", [P, ROWS, PACK], BF16)
+        dst, src = interleaved(g_grouped, g_raw)
+        nc.vector.tensor_copy(dst, src)
+        neg_max = tile("neg_max", [P, 1], F32)
+        nc.vector.tensor_reduce(neg_max[:], logp[:], mybir.AxisListType.X, ALU.max, negate=True)
+        g_mx = quantize("g", g_grouped)
+        product(c_ps[:], g_mx, val_codes[:], val_scales[:], True, True)
+        half_logpr = tile("half_logpr", [P, SLOTS], F32)
+        nc.vector.scalar_tensor_tensor(half_logpr[:], a_ps[:], 0.25, logden[:], ALU.mult, ALU.subtract)
+        u = tile("u", [P, SLOTS], F32)
+        nc.vector.tensor_scalar(u[:], u0[:], sharp256[:], 256.0, ALU.mult, ALU.add)
+
+        p = tile("p", [P, SLOTS], F32)
+        z = tile("z", [P, 1], F32)
+        nc.scalar.activation(out=p[:], in_=logp[:], func=ACT.Exp, bias=neg_max[:], accum_out=z[:])
+        rz = tile("rz", [P, 1], F32)
+        nc.vector.reciprocal(rz[:], z[:])
+        cp = tile("cp", [P, SLOTS], F32)
+        neg_s = tile("neg_s", [P, 1], F32)
+        nc.vector.scalar_tensor_tensor(cp[:], c_ps[:], -1.0, p[:], ALU.mult, ALU.mult, accum_out=neg_s[:])
+
+        pr = tile("pr", [P, SLOTS], F32)
+        rz2 = tile("rz2", [P, 1], F32)
+        nc.scalar.activation(out=pr[:, lower], in_=half_logpr[:, lower], func=ACT.Exp, scale=2.0, bias=neg_max[:])
+        nc.scalar.activation(out=rz2[:], in_=rz[:], func=ACT.Square)
+        nc.scalar.activation(out=pr[:, upper], in_=half_logpr[:, upper], func=ACT.Exp, scale=2.0, bias=neg_max[:])
+        slope = tile("slope", [P, SLOTS], F32)
+        centred = tile("centred", [P, SLOTS], F32)
+        for cols in (lower, upper):
+            nc.scalar.activation(
+                out=centred[:, cols], in_=c_ps[:, cols], func=ACT.Identity, scale=z[:], bias=neg_s[:]
+            )
+        for cols in (lower, upper):
+            nc.vector.scalar_tensor_tensor(slope[:, cols], pr[:, cols], rz2[:], u[:, cols], ALU.mult, ALU.mult)
+        for h, cols in enumerate((lower, upper)):
+            nc.vector.tensor_tensor(
+                window[:].indirect(offsets[:, h * LIST_COLS // 2 : (h + 1) * LIST_COLS // 2]),
+                slope[:, cols],
+                centred[:, cols],
+                ALU.mult,
+            )
+
+        c0 = 0
+        for n, width in enumerate(OUT_CHUNKS):
+            cols = slice(c0, c0 + width)
+            res = tile("res%d" % n, [P, width], F32)
+            nc.vector.tensor_tensor(res[:], window[:, cols], old_sb[:, cols], ALU.add)
+            nc.sync.dma_start(out=out[:, cols], in_=res[:])
+            c0 = c0 + width

@@ -40,10 +40,10 @@ def tile_attend_balikescores_s_kernel(
         def load_words(queue, dst, words):
             queue.dma_start(out=dst[:].bitcast(I32), in_=words[0].rearrange("p n t -> p (n t)").bitcast(I32))
 
-        def load_scale_rows(queues, dst, scales):
+        def load_scale_rows(queue, dst, scales):
             rows = scales[0].bitcast(I32).rearrange("(quad j) c -> j quad c", j=4)
             for j in range(4):
-                queues[j].dma_start(out=dst[:].bitcast(I32)[j:P:32, :], in_=rows[j])
+                queue.dma_start(out=dst[:].bitcast(I32)[j:P:32, :], in_=rows[j])
 
         def load_rows(queue, dst, src):
             queue.dma_start(out=dst[:], in_=src.rearrange("(p t) q -> p t q", t=PACK))
@@ -74,49 +74,47 @@ def tile_attend_balikescores_s_kernel(
             )
 
         offsets = tile("offsets", [P, LIST_COLS], U16)
-        key_pool = tile("key_pool", [P, T], U32)
         key_scale_pool = tile("key_scale_pool", [P, T], U8)
-        val_scale_pool = tile("val_scale_pool", [P, T], U8)
         q_raw = tile("q_raw", [P, PACK, ROWS], F32)
         q2_raw = tile("q2_raw", [P, PACK, ROWS], F32)
-        sharp_col = tile("sharp_col", [P, 1], F32)
+        g_raw = tile("g_raw", [P, PACK, ROWS], F32)
         window = tile("window", [P, T], F32)
         one = tile("one", [P, 1], F32)
         warm = tile("warm", [P, 1], F32)
 
-        nc.vector.memset(key_scale_pool[:].bitcast(I32), 0)
-        nc.vector.memset(val_scale_pool[:].bitcast(I32), 0)
-        nc.gpsimd.memset(one[:], 1.0)
-        nc.scalar.activation(out=warm[:], in_=one[:], func=ACT.Ln, bias=one[:])
-
         nc.sync.dma_start(offsets[:], offs)
-        load_rows(nc.scalar, q_raw, query)
-        load_rows(nc.scalar, q2_raw, query2)
-        load_words(nc.scalar, key_pool, keys_words)
-        load_scale_rows((nc.sync,) * 4, key_scale_pool, keys_scales)
-        load_scale_rows((nc.sync,) * 3 + (nc.gpsimd,), val_scale_pool, vals_scales)
-        nc.gpsimd.dma_start(out=sharp_col[:], in_=sharp)
+        load_rows(nc.sync, q_raw, query)
+        load_rows(nc.sync, q2_raw, query2)
+        load_rows(nc.sync, g_raw, gout)
+        nc.vector.memset(key_scale_pool[:].bitcast(I32), 0)
+        load_scale_rows(nc.sync, key_scale_pool, keys_scales)
+        nc.gpsimd.memset(one[:], 1.0)
+        nc.scalar.activation(out=warm[:], in_=one[:], func=ACT.Ln)
+        key_pool = tile("key_pool", [P, T], U32, tag="warm")
+        load_words(nc.sync, key_pool, keys_words)
+        sharp_col = tile("sharp_col", [P, 1], F32, tag="one")
+        nc.scalar.dma_start(out=sharp_col[:], in_=sharp)
         nc.vector.memset(window[:], 0.0)
-
-        key_scales = tile("key_scales", [P, SLOTS], U8)
-        nc.vector.tensor_copy(key_scales[:], key_scale_pool[:].indirect(offsets[:]))
 
         q_grouped = tile("q_grouped", [P, ROWS, PACK], BF16)
         nq2_grouped = tile("nq2_grouped", [P, ROWS, PACK], BF16)
+        g_grouped = tile("g_grouped", [P, ROWS, PACK], BF16)
         dst, src = interleaved(q_grouped, q_raw)
         nc.scalar.activation(out=dst, in_=src, func=ACT.Copy)
+        val_scale_pool = tile("val_scale_pool", [P, T], U8, tag="q_raw")
+        nc.vector.memset(val_scale_pool[:].bitcast(I32), 0)
+        load_scale_rows(nc.sync, val_scale_pool, vals_scales)
+        q_mx = quantize("q", q_grouped)
         dst, src = interleaved(nq2_grouped, q2_raw)
         nc.scalar.activation(out=dst, in_=src, func=ACT.Copy, scale=-1.0)
-        g_raw = tile("g_raw", [P, PACK, ROWS], F32, tag="q_raw")
-        load_rows(nc.sync, g_raw, gout)
         val_pool = tile("val_pool", [P, T], U32, tag="q2_raw")
-        load_words(nc.scalar, val_pool, vals_words)
-        q_mx = quantize("q", q_grouped)
-        val_scales = tile("val_scales", [P, SLOTS], U8)
-        nc.vector.tensor_copy(val_scales[:], val_scale_pool[:].indirect(offsets[:]))
+        load_words(nc.sync, val_pool, vals_words)
+        dst, src = interleaved(g_grouped, g_raw)
+        nc.scalar.activation(out=dst, in_=src, func=ACT.Copy)
+        key_scales = tile("key_scales", [P, SLOTS], U8)
+        nc.vector.tensor_copy(key_scales[:], key_scale_pool[:].indirect(offsets[:]))
         nq2_mx = quantize("nq2", nq2_grouped)
-        sharp256 = tile("sharp256", [P, 1], F32)
-        nc.vector.tensor_scalar(sharp256[:], sharp_col[:], 256.0, None, ALU.mult)
+        g_mx = quantize("g", g_grouped)
 
         key_codes = []
         for h in range(2):
@@ -126,7 +124,7 @@ def tile_attend_balikescores_s_kernel(
             )
             key_codes.append(codes)
 
-        old_sb = tile("old_sb", [P, T], F32, tag="key_pool")
+        old_sb = tile("old_sb", [P, T], F32, tag="warm")
         nc.sync.dma_start(out=old_sb[:], in_=old)
 
         a_ps = ps.tile([P, SLOTS], F32, name="a_ps")
@@ -155,51 +153,49 @@ def tile_attend_balikescores_s_kernel(
         product(a_ps[:, upper], q_mx, key_codes[1][:], key_scales[:, upper], True, True)
         nc.scalar.activation(out=sq[:, second], in_=d1_ps[:], func=ACT.Square)
         nc.scalar.activation(out=sq[:, first], in_=d0[:], func=ACT.Square)
-        nc.scalar.activation(out=logden[:, lower], in_=sq[:, lower], func=ACT.Ln, scale=sharp_col[:], bias=one[:])
+        nc.scalar.activation(out=logden[:, lower], in_=sq[:, lower], func=ACT.Ln, scale=sharp_col[:], bias=1.0)
         nc.scalar.activation(out=sq[:, upper], in_=d2_ps[:], func=ACT.Square)
-        nc.scalar.activation(out=logden[:, upper], in_=sq[:, upper], func=ACT.Ln, scale=sharp_col[:], bias=one[:])
+        nc.scalar.activation(out=logden[:, upper], in_=sq[:, upper], func=ACT.Ln, scale=sharp_col[:], bias=1.0)
 
-        u0 = tile("u0", [P, SLOTS], F32)
-        for cols, dl in ((second, d1_ps), (first, d0), (upper, d2_ps)):
-            nc.vector.scalar_tensor_tensor(u0[:, cols], dl[:], -4.0, sq[:, cols], ALU.mult, ALU.add)
-        val_codes = tile("val_codes", [P, SLOTS], U32)
-        nc.vector.tensor_copy(val_codes[:], val_pool[:].indirect(offsets[:]))
+        val_scales = tile("val_scales", [P, SLOTS], U8, tag="nb")
+        nc.vector.tensor_copy(val_scales[:], val_scale_pool[:].indirect(offsets[:]))
         logp = tile("logp", [P, SLOTS], F32)
         nc.vector.scalar_tensor_tensor(logp[:], a_ps[:], 0.5, logden[:], ALU.mult, ALU.subtract)
-        g_grouped = tile("g_grouped", [P, ROWS, PACK], BF16)
-        dst, src = interleaved(g_grouped, g_raw)
-        nc.vector.tensor_copy(dst, src)
-        neg_max = tile("neg_max", [P, 1], F32)
-        nc.vector.tensor_reduce(neg_max[:], logp[:], mybir.AxisListType.X, ALU.max, negate=True)
-        g_mx = quantize("g", g_grouped)
+        val_codes = tile("val_codes", [P, SLOTS], U32)
+        nc.vector.tensor_copy(val_codes[:], val_pool[:].indirect(offsets[:]))
         product(c_ps[:], g_mx, val_codes[:], val_scales[:], True, True)
-        half_logpr = tile("half_logpr", [P, SLOTS], F32)
-        nc.vector.scalar_tensor_tensor(half_logpr[:], a_ps[:], 0.25, logden[:], ALU.mult, ALU.subtract)
-        u = tile("u", [P, SLOTS], F32)
-        nc.vector.tensor_scalar(u[:], u0[:], sharp256[:], 256.0, ALU.mult, ALU.add)
+        late = tile("late", [P, SLOTS + 16], F32, tag="q2_raw")
+        neg_max = late[:, SLOTS : SLOTS + 1]
+        pull = late[:, :SLOTS]
+        nc.vector.tensor_reduce(neg_max, logp[:], mybir.AxisListType.X, ALU.max, negate=True)
 
+        r = tile("r", [P, SLOTS], F32, tag="sq")
+        for cols in (upper, lower):
+            nc.scalar.activation(out=r[:, cols], in_=logden[:, cols], func=ACT.Exp, scale=-1.0)
         p = tile("p", [P, SLOTS], F32)
         z = tile("z", [P, 1], F32)
-        nc.scalar.activation(out=p[:], in_=logp[:], func=ACT.Exp, bias=neg_max[:], accum_out=z[:])
+        nc.scalar.activation(out=p[:], in_=logp[:], func=ACT.Exp, bias=neg_max, accum_out=z[:])
+        for cols, dl in ((upper, d2_ps), (first, d0), (second, d1_ps)):
+            nc.vector.scalar_tensor_tensor(pull[:, cols], dl[:], sharp_col[:], r[:, cols], ALU.mult, ALU.mult)
         rz = tile("rz", [P, 1], F32)
         nc.vector.reciprocal(rz[:], z[:])
         cp = tile("cp", [P, SLOTS], F32)
         neg_s = tile("neg_s", [P, 1], F32)
-        nc.vector.scalar_tensor_tensor(cp[:], c_ps[:], -1.0, p[:], ALU.mult, ALU.mult, accum_out=neg_s[:])
-
-        pr = tile("pr", [P, SLOTS], F32)
+        nc.vector.scalar_tensor_tensor(cp[:], c_ps[:], 1024.0, p[:], ALU.mult, ALU.mult, accum_out=neg_s[:])
+        gain = tile("gain", [P, 1], F32)
         rz2 = tile("rz2", [P, 1], F32)
-        nc.scalar.activation(out=pr[:, lower], in_=half_logpr[:, lower], func=ACT.Exp, scale=2.0, bias=neg_max[:])
+        shift = tile("shift", [P, 1], F32)
+        nc.scalar.activation(out=gain[:], in_=rz[:], func=ACT.Copy, scale=-1024.0)
         nc.scalar.activation(out=rz2[:], in_=rz[:], func=ACT.Square)
-        nc.scalar.activation(out=pr[:, upper], in_=half_logpr[:, upper], func=ACT.Exp, scale=2.0, bias=neg_max[:])
+        nc.scalar.activation(out=shift[:], in_=neg_s[:], func=ACT.Copy, scale=rz2[:])
         slope = tile("slope", [P, SLOTS], F32)
         centred = tile("centred", [P, SLOTS], F32)
         for cols in (lower, upper):
             nc.scalar.activation(
-                out=centred[:, cols], in_=c_ps[:, cols], func=ACT.Identity, scale=z[:], bias=neg_s[:]
+                out=centred[:, cols], in_=c_ps[:, cols], func=ACT.Identity, scale=gain[:], bias=shift[:]
             )
         for cols in (lower, upper):
-            nc.vector.scalar_tensor_tensor(slope[:, cols], pr[:, cols], rz2[:], u[:, cols], ALU.mult, ALU.mult)
+            nc.vector.scalar_tensor_tensor(slope[:, cols], pull[:, cols], -0.25, p[:, cols], ALU.add, ALU.mult)
         for h, cols in enumerate((lower, upper)):
             nc.vector.tensor_tensor(
                 window[:].indirect(offsets[:, h * LIST_COLS // 2 : (h + 1) * LIST_COLS // 2]),

@@ -21,7 +21,10 @@ ROWS = 128
 HALF = SLOTS // 2
 QUARTER = SLOTS // 4
 LIST_COLS = SLOTS // 16
-OUT_CHUNKS = (512, 512, 512, 512)
+QUAD = 32
+SCALE_ROWS = 4
+CHUNK = 512
+PAD = 16
 
 FLOPS = 3 * 2 * K * ROWS * SLOTS
 
@@ -37,21 +40,24 @@ def tile_attend_balikescores_s_kernel(
         def tile(name, shape, dtype, tag=None):
             return sb.tile(shape, dtype, name=name, tag=tag or name, align_bytes=64)
 
-        def load_words(queue, dst, words):
-            queue.dma_start(out=dst[:].bitcast(I32), in_=words[0].rearrange("p n t -> p (n t)").bitcast(I32))
+        def load_words(dst, words):
+            nc.sync.dma_start(out=dst[:].bitcast(I32), in_=words[0].rearrange("p n t -> p (n t)").bitcast(I32))
 
-        def load_scale_rows(queue, dst, scales):
-            rows = scales[0].bitcast(I32).rearrange("(quad j) c -> j quad c", j=4)
-            for j in range(4):
-                queue.dma_start(out=dst[:].bitcast(I32)[j:P:32, :], in_=rows[j])
+        def load_scale_rows(dst, scales):
+            nc.vector.memset(dst[:].bitcast(I32), 0)
+            rows = scales[0].bitcast(I32).rearrange("(quad j) c -> j quad c", j=SCALE_ROWS)
+            for j in range(SCALE_ROWS):
+                nc.sync.dma_start(out=dst[:].bitcast(I32)[j:P:QUAD, :], in_=rows[j])
 
-        def load_rows(queue, dst, src):
-            queue.dma_start(out=dst[:], in_=src.rearrange("(p t) q -> p t q", t=PACK))
+        def load_rows(dst, src):
+            nc.sync.dma_start(out=dst[:], in_=src.rearrange("(p t) q -> p t q", t=PACK))
 
-        def interleaved(grouped, raw):
-            return (
-                grouped[:].rearrange("p (c i) t -> p c t i", i=4),
-                raw[:].rearrange("p t (c i) -> p c t i", i=4),
+        def round_and_interleave(grouped, raw, sign):
+            nc.scalar.activation(
+                out=grouped[:].rearrange("p (c i) t -> p c t i", i=4),
+                in_=raw[:].rearrange("p t (c i) -> p c t i", i=4),
+                func=ACT.Copy,
+                scale=sign,
             )
 
         def quantize(name, grouped):
@@ -62,152 +68,148 @@ def tile_attend_balikescores_s_kernel(
             )
             return codes, scales
 
-        def product(dst, rows_operand, codes, scales, start, stop):
+        def product(dst, rows_mx, codes, scales, start, stop):
             nc.tensor.matmul_mx(
                 out=dst,
-                lhsT=rows_operand[0][:].bitcast(FP8X4),
-                lhsT_scale=rows_operand[1][:],
+                lhsT=rows_mx[0][:].bitcast(FP8X4),
+                lhsT_scale=rows_mx[1][:],
                 rhs=codes.bitcast(FP8X4),
                 rhs_scale=scales,
                 start=start,
                 stop=stop,
             )
 
-        offsets = tile("offsets", [P, LIST_COLS], U16)
-        key_scale_pool = tile("key_scale_pool", [P, T], U8)
-        q_raw = tile("q_raw", [P, PACK, ROWS], F32)
-        q2_raw = tile("q2_raw", [P, PACK, ROWS], F32)
-        g_raw = tile("g_raw", [P, PACK, ROWS], F32)
-        window = tile("window", [P, T], F32)
-        one = tile("one", [P, 1], F32)
-        warm = tile("warm", [P, 1], F32)
+        def list_half(h):
+            return offsets[:, h * LIST_COLS // 2 : (h + 1) * LIST_COLS // 2]
 
-        nc.sync.dma_start(offsets[:], offs)
-        load_rows(nc.sync, q_raw, query)
-        load_rows(nc.sync, q2_raw, query2)
-        load_rows(nc.sync, g_raw, gout)
-        nc.vector.memset(key_scale_pool[:].bitcast(I32), 0)
-        load_scale_rows(nc.sync, key_scale_pool, keys_scales)
-        nc.gpsimd.memset(one[:], 1.0)
-        nc.scalar.activation(out=warm[:], in_=one[:], func=ACT.Ln)
-        key_pool = tile("key_pool", [P, T], U32, tag="warm")
-        load_words(nc.sync, key_pool, keys_words)
-        sharp_col = tile("sharp_col", [P, 1], F32, tag="one")
-        nc.scalar.dma_start(out=sharp_col[:], in_=sharp)
-        nc.vector.memset(window[:], 0.0)
-
-        q_grouped = tile("q_grouped", [P, ROWS, PACK], BF16)
-        nq2_grouped = tile("nq2_grouped", [P, ROWS, PACK], BF16)
-        g_grouped = tile("g_grouped", [P, ROWS, PACK], BF16)
-        dst, src = interleaved(q_grouped, q_raw)
-        nc.scalar.activation(out=dst, in_=src, func=ACT.Copy)
-        val_scale_pool = tile("val_scale_pool", [P, T], U8, tag="q_raw")
-        nc.vector.memset(val_scale_pool[:].bitcast(I32), 0)
-        load_scale_rows(nc.sync, val_scale_pool, vals_scales)
-        q_mx = quantize("q", q_grouped)
-        dst, src = interleaved(nq2_grouped, q2_raw)
-        nc.scalar.activation(out=dst, in_=src, func=ACT.Copy, scale=-1.0)
-        val_pool = tile("val_pool", [P, T], U32, tag="q2_raw")
-        load_words(nc.sync, val_pool, vals_words)
-        dst, src = interleaved(g_grouped, g_raw)
-        nc.scalar.activation(out=dst, in_=src, func=ACT.Copy)
-        key_scales = tile("key_scales", [P, SLOTS], U8)
-        nc.vector.tensor_copy(key_scales[:], key_scale_pool[:].indirect(offsets[:]))
-        nq2_mx = quantize("nq2", nq2_grouped)
-        g_mx = quantize("g", g_grouped)
-
-        key_codes = []
-        for h in range(2):
-            codes = tile("key_codes%d" % h, [P, HALF], U32)
-            nc.vector.tensor_copy(
-                codes[:], key_pool[:].indirect(offsets[:, h * LIST_COLS // 2 : (h + 1) * LIST_COLS // 2])
-            )
-            key_codes.append(codes)
-
-        old_sb = tile("old_sb", [P, T], F32, tag="warm")
-        nc.sync.dma_start(out=old_sb[:], in_=old)
-
-        a_ps = ps.tile([P, SLOTS], F32, name="a_ps")
-        nb_ps = ps.tile([P, QUARTER], F32, name="nb_ps")
-        d1_ps = ps.tile([P, QUARTER], F32, name="d1_ps")
-        d2_ps = ps.tile([P, HALF], F32, name="d2_ps")
-        c_ps = ps.tile([P, SLOTS], F32, name="c_ps")
         first = slice(0, QUARTER)
         second = slice(QUARTER, HALF)
         lower = slice(0, HALF)
         upper = slice(HALF, SLOTS)
 
+        offsets = tile("offsets", [P, LIST_COLS], U16)
+        q_raw = tile("q_raw", [P, PACK, ROWS], F32)
+        q2_raw = tile("q2_raw", [P, PACK, ROWS], F32)
+        key_scale_pool = tile("key_scale_pool", [P, T], U8)
+        nc.sync.dma_start(offsets[:], offs)
+        load_rows(q_raw, query)
+        load_rows(q2_raw, query2)
+        load_scale_rows(key_scale_pool, keys_scales)
+
+        one = tile("one", [P, 1], F32)
+        warm = tile("warm", [P, 1], F32)
+        nc.gpsimd.memset(one[:], 1.0)
+        nc.scalar.activation(out=warm[:], in_=one[:], func=ACT.Ln)
+
+        key_pool = tile("key_pool", [P, T], U32, tag="warm")
+        load_words(key_pool, keys_words)
+        sharp_col = tile("sharp_col", [P, 1], F32, tag="one")
+        nc.scalar.dma_start(out=sharp_col[:], in_=sharp)
+
+        window = tile("window", [P, T], F32)
+        nc.vector.memset(window[:], 0.0)
+
+        q_grouped = tile("q_grouped", [P, ROWS, PACK], BF16)
+        nq2_grouped = tile("nq2_grouped", [P, ROWS, PACK], BF16)
+        g_grouped = tile("g_grouped", [P, ROWS, PACK], BF16)
+        round_and_interleave(q_grouped, q_raw, 1.0)
+        g_raw = tile("g_raw", [P, PACK, ROWS], F32, tag="q_raw")
+        load_rows(g_raw, gout)
+        q_mx = quantize("q", q_grouped)
+        val_scale_pool = tile("val_scale_pool", [P, T], U8, tag="q_grouped")
+        load_scale_rows(val_scale_pool, vals_scales)
+        round_and_interleave(nq2_grouped, q2_raw, -1.0)
+        nq2_mx = quantize("nq2", nq2_grouped)
+        val_pool = tile("val_pool", [P, T], U32, tag="nq2_grouped")
+        load_words(val_pool, vals_words)
+        key_scales = tile("key_scales", [P, SLOTS], U8)
+        nc.vector.tensor_copy(key_scales[:], key_scale_pool[:].indirect(offsets[:]))
+        round_and_interleave(g_grouped, g_raw, 1.0)
+
+        key_codes = []
+        for h in range(2):
+            codes = tile("key_codes%d" % h, [P, HALF], U32)
+            nc.vector.tensor_copy(codes[:], key_pool[:].indirect(list_half(h)))
+            key_codes.append(codes)
+        old_sb = tile("old_sb", [P, T], F32, tag="warm")
+        nc.sync.dma_start(out=old_sb[:], in_=old)
+
+        a_ps = ps.tile([P, SLOTS], F32, name="a_ps")
+        nb_ps = ps.tile([P, QUARTER], F32, name="nb_ps")
+        dl_second = ps.tile([P, QUARTER], F32, name="dl_second")
+        dl_upper = ps.tile([P, HALF], F32, name="dl_upper")
+        c_ps = ps.tile([P, SLOTS], F32, name="c_ps")
         product(nb_ps[:], nq2_mx, key_codes[0][:, first], key_scales[:, first], True, True)
-        product(a_ps[:, lower], q_mx, key_codes[0][:], key_scales[:, lower], True, True)
-        product(d1_ps[:], q_mx, key_codes[0][:, second], key_scales[:, second], True, False)
-        product(d1_ps[:], nq2_mx, key_codes[0][:, second], key_scales[:, second], False, True)
-        product(d2_ps[:], nq2_mx, key_codes[1][:], key_scales[:, upper], True, False)
-        product(d2_ps[:], q_mx, key_codes[1][:], key_scales[:, upper], False, True)
+        product(a_ps[:, first], q_mx, key_codes[0][:, first], key_scales[:, first], True, True)
+        product(dl_second[:], q_mx, key_codes[0][:, second], key_scales[:, second], True, False)
+        product(dl_second[:], nq2_mx, key_codes[0][:, second], key_scales[:, second], False, True)
+        product(dl_upper[:], nq2_mx, key_codes[1][:], key_scales[:, upper], True, False)
+        product(dl_upper[:], q_mx, key_codes[1][:], key_scales[:, upper], False, True)
 
         nb = tile("nb", [P, QUARTER], F32)
-        d0 = tile("d0", [P, QUARTER], F32)
+        dl_first = tile("dl_first", [P, QUARTER], F32)
+        nc.scalar.copy(nb[:], nb_ps[:])
+        nc.vector.tensor_tensor(dl_first[:], a_ps[:, first], nb[:], ALU.add)
+        product(a_ps[:, second], q_mx, key_codes[0][:, second], key_scales[:, second], True, True)
+        product(a_ps[:, upper], q_mx, key_codes[1][:], key_scales[:, upper], True, True)
+
         sq = tile("sq", [P, SLOTS], F32)
         logden = tile("logden", [P, SLOTS], F32)
-        nc.scalar.copy(nb[:], nb_ps[:])
-        nc.vector.tensor_tensor(d0[:], a_ps[:, first], nb[:], ALU.add)
-        product(a_ps[:, upper], q_mx, key_codes[1][:], key_scales[:, upper], True, True)
-        nc.scalar.activation(out=sq[:, second], in_=d1_ps[:], func=ACT.Square)
-        nc.scalar.activation(out=sq[:, first], in_=d0[:], func=ACT.Square)
-        nc.scalar.activation(out=logden[:, lower], in_=sq[:, lower], func=ACT.Ln, scale=sharp_col[:], bias=1.0)
-        nc.scalar.activation(out=sq[:, upper], in_=d2_ps[:], func=ACT.Square)
-        nc.scalar.activation(out=logden[:, upper], in_=sq[:, upper], func=ACT.Ln, scale=sharp_col[:], bias=1.0)
+        for cols, dl in ((second, dl_second), (first, dl_first), (upper, dl_upper)):
+            nc.scalar.activation(out=sq[:, cols], in_=dl[:], func=ACT.Square)
+        nc.scalar.activation(out=logden[:], in_=sq[:], func=ACT.Ln, scale=sharp_col[:], bias=1.0)
 
         val_scales = tile("val_scales", [P, SLOTS], U8, tag="nb")
         nc.vector.tensor_copy(val_scales[:], val_scale_pool[:].indirect(offsets[:]))
-        logp = tile("logp", [P, SLOTS], F32)
-        nc.vector.scalar_tensor_tensor(logp[:], a_ps[:], 0.5, logden[:], ALU.mult, ALU.subtract)
+        g_mx = quantize("g", g_grouped)
+
+        neg_half_a = tile("neg_half_a", [P, SLOTS], F32, tag="q_grouped")
+        neg_max = tile("neg_max", [P, 1], F32)
+        nc.vector.tensor_scalar(neg_half_a[:], a_ps[:], -0.5, None, ALU.mult, ALU.min, accum_out=neg_max[:])
+
         val_codes = tile("val_codes", [P, SLOTS], U32)
         nc.vector.tensor_copy(val_codes[:], val_pool[:].indirect(offsets[:]))
         product(c_ps[:], g_mx, val_codes[:], val_scales[:], True, True)
-        late = tile("late", [P, SLOTS + 16], F32, tag="q2_raw")
-        neg_max = late[:, SLOTS : SLOTS + 1]
-        pull = late[:, :SLOTS]
-        nc.vector.tensor_reduce(neg_max, logp[:], mybir.AxisListType.X, ALU.max, negate=True)
+
+        behind_vals = tile("behind_vals", [P, 2 * SLOTS + PAD], F32, tag="nq2_grouped")
+        neg_logp = behind_vals[:, :SLOTS]
+        pull = behind_vals[:, SLOTS : 2 * SLOTS]
+        rz = behind_vals[:, 2 * SLOTS : 2 * SLOTS + 1]
+        nc.vector.tensor_tensor(neg_logp, neg_half_a[:], logden[:], ALU.add)
 
         r = tile("r", [P, SLOTS], F32, tag="sq")
         for cols in (upper, lower):
             nc.scalar.activation(out=r[:, cols], in_=logden[:, cols], func=ACT.Exp, scale=-1.0)
         p = tile("p", [P, SLOTS], F32)
         z = tile("z", [P, 1], F32)
-        nc.scalar.activation(out=p[:], in_=logp[:], func=ACT.Exp, bias=neg_max, accum_out=z[:])
-        for cols, dl in ((upper, d2_ps), (first, d0), (second, d1_ps)):
+        nc.scalar.activation(out=p[:], in_=neg_logp, func=ACT.Exp, scale=-1.0, bias=neg_max[:], accum_out=z[:])
+        for cols, dl in ((upper, dl_upper), (first, dl_first), (second, dl_second)):
             nc.vector.scalar_tensor_tensor(pull[:, cols], dl[:], sharp_col[:], r[:, cols], ALU.mult, ALU.mult)
-        rz = tile("rz", [P, 1], F32)
-        nc.vector.reciprocal(rz[:], z[:])
-        cp = tile("cp", [P, SLOTS], F32)
+
+        neg_cp = tile("neg_cp", [P, SLOTS], F32)
         neg_s = tile("neg_s", [P, 1], F32)
-        nc.vector.scalar_tensor_tensor(cp[:], c_ps[:], 1024.0, p[:], ALU.mult, ALU.mult, accum_out=neg_s[:])
-        gain = tile("gain", [P, 1], F32)
-        rz2 = tile("rz2", [P, 1], F32)
-        shift = tile("shift", [P, 1], F32)
-        nc.scalar.activation(out=gain[:], in_=rz[:], func=ACT.Copy, scale=-1024.0)
-        nc.scalar.activation(out=rz2[:], in_=rz[:], func=ACT.Square)
-        nc.scalar.activation(out=shift[:], in_=neg_s[:], func=ACT.Copy, scale=rz2[:])
-        slope = tile("slope", [P, SLOTS], F32)
+        nc.vector.scalar_tensor_tensor(neg_cp[:], c_ps[:], -1.0, p[:], ALU.mult, ALU.mult, accum_out=neg_s[:])
+
         centred = tile("centred", [P, SLOTS], F32)
+        slope = tile("slope", [P, SLOTS], F32)
         for cols in (lower, upper):
             nc.scalar.activation(
-                out=centred[:, cols], in_=c_ps[:, cols], func=ACT.Identity, scale=gain[:], bias=shift[:]
+                out=centred[:, cols], in_=c_ps[:, cols], func=ACT.Identity, scale=z[:], bias=neg_s[:]
             )
         for cols in (lower, upper):
             nc.vector.scalar_tensor_tensor(slope[:, cols], pull[:, cols], -0.25, p[:, cols], ALU.add, ALU.mult)
+        nc.vector.reciprocal(rz, z[:])
+        gain = tile("gain", [P, 1], F32)
+        row_factor = tile("row_factor", [P, 1], F32)
+        nc.scalar.activation(out=gain[:], in_=rz, func=ACT.Copy, scale=-1024.0)
+        nc.scalar.activation(out=row_factor[:], in_=gain[:], func=ACT.Copy, scale=rz)
         for h, cols in enumerate((lower, upper)):
-            nc.vector.tensor_tensor(
-                window[:].indirect(offsets[:, h * LIST_COLS // 2 : (h + 1) * LIST_COLS // 2]),
-                slope[:, cols],
-                centred[:, cols],
-                ALU.mult,
-            )
+            nc.vector.tensor_tensor(window[:].indirect(list_half(h)), slope[:, cols], centred[:, cols], ALU.mult)
 
-        c0 = 0
-        for n, width in enumerate(OUT_CHUNKS):
-            cols = slice(c0, c0 + width)
-            res = tile("res%d" % n, [P, width], F32)
-            nc.vector.tensor_tensor(res[:], window[:, cols], old_sb[:, cols], ALU.add)
+        for n in range(T // CHUNK):
+            cols = slice(n * CHUNK, (n + 1) * CHUNK)
+            res = tile("res%d" % n, [P, CHUNK], F32)
+            nc.vector.scalar_tensor_tensor(
+                res[:], window[:, cols], row_factor[:], old_sb[:, cols], ALU.mult, ALU.add
+            )
             nc.sync.dma_start(out=out[:, cols], in_=res[:])
-            c0 = c0 + width

from contextlib import ExitStack

import concourse.mybir as mybir

F32 = mybir.dt.float32
BF16 = mybir.dt.bfloat16
I32 = mybir.dt.int32
U32 = mybir.dt.uint32
U16 = mybir.dt.uint16
U8 = mybir.dt.uint8
FP8X4 = mybir.dt.float8_e4m3fn_x4
ALU = mybir.AluOpType
ACT = mybir.ActivationFunctionType

P = 128
PACK = 4
K = P * PACK
T = 2048
SLOTS = 512
ROWS = 128
HALF = SLOTS // 2
QUARTER = SLOTS // 4
LIST_COLS = SLOTS // 16
QUAD = 32
SCALE_ROWS = 4
CHUNK = 512
PAD = 16

FLOPS = 3 * 2 * K * ROWS * SLOTS


def tile_attend_balikescores_s_kernel(
    tc, query, query2, keys_words, keys_scales, sharp, gout, vals_words, vals_scales, old, offs, out
):
    nc = tc.nc
    with ExitStack() as ctx:
        sb = ctx.enter_context(tc.tile_pool(name="sb", bufs=1))
        ps = ctx.enter_context(tc.psum_pool(name="ps", bufs=1))

        def tile(name, shape, dtype, tag=None):
            return sb.tile(shape, dtype, name=name, tag=tag or name, align_bytes=64)

        def load_words(dst, words):
            nc.sync.dma_start(out=dst[:].bitcast(I32), in_=words[0].rearrange("p n t -> p (n t)").bitcast(I32))

        def load_scale_rows(dst, scales):
            nc.vector.memset(dst[:].bitcast(I32), 0)
            rows = scales[0].bitcast(I32).rearrange("(quad j) c -> j quad c", j=SCALE_ROWS)
            for j in range(SCALE_ROWS):
                nc.sync.dma_start(out=dst[:].bitcast(I32)[j:P:QUAD, :], in_=rows[j])

        def load_rows(dst, src):
            nc.sync.dma_start(out=dst[:], in_=src.rearrange("(p t) q -> p t q", t=PACK))

        def round_and_interleave(grouped, raw, sign):
            nc.scalar.activation(
                out=grouped[:].rearrange("p (c i) t -> p c t i", i=4),
                in_=raw[:].rearrange("p t (c i) -> p c t i", i=4),
                func=ACT.Copy,
                scale=sign,
            )

        def quantize(name, grouped):
            codes = tile(name + "_codes", [P, ROWS], U32)
            scales = tile(name + "_scales", [P, ROWS], U8)
            nc.vector.quantize_mx(
                out=codes[:].bitcast(FP8X4), scales=scales[:], in_=grouped[:].rearrange("p q t -> p (q t)")
            )
            return codes, scales

        def product(dst, rows_mx, codes, scales, start, stop):
            nc.tensor.matmul_mx(
                out=dst,
                lhsT=rows_mx[0][:].bitcast(FP8X4),
                lhsT_scale=rows_mx[1][:],
                rhs=codes.bitcast(FP8X4),
                rhs_scale=scales,
                start=start,
                stop=stop,
            )

        def list_half(h):
            return offsets[:, h * LIST_COLS // 2 : (h + 1) * LIST_COLS // 2]

        first = slice(0, QUARTER)
        second = slice(QUARTER, HALF)
        lower = slice(0, HALF)
        upper = slice(HALF, SLOTS)

        offsets = tile("offsets", [P, LIST_COLS], U16)
        q_raw = tile("q_raw", [P, PACK, ROWS], F32)
        q2_raw = tile("q2_raw", [P, PACK, ROWS], F32)
        key_scale_pool = tile("key_scale_pool", [P, T], U8)
        nc.sync.dma_start(offsets[:], offs)
        load_rows(q_raw, query)
        load_rows(q2_raw, query2)
        load_scale_rows(key_scale_pool, keys_scales)

        one = tile("one", [P, 1], F32)
        warm = tile("warm", [P, 1], F32)
        nc.gpsimd.memset(one[:], 1.0)
        nc.scalar.activation(out=warm[:], in_=one[:], func=ACT.Ln)

        key_pool = tile("key_pool", [P, T], U32, tag="warm")
        load_words(key_pool, keys_words)
        sharp_col = tile("sharp_col", [P, 1], F32, tag="one")
        nc.scalar.dma_start(out=sharp_col[:], in_=sharp)

        window = tile("window", [P, T], F32)
        nc.vector.memset(window[:], 0.0)

        q_grouped = tile("q_grouped", [P, ROWS, PACK], BF16)
        nq2_grouped = tile("nq2_grouped", [P, ROWS, PACK], BF16)
        g_grouped = tile("g_grouped", [P, ROWS, PACK], BF16)
        round_and_interleave(q_grouped, q_raw, 1.0)
        g_raw = tile("g_raw", [P, PACK, ROWS], F32, tag="q_raw")
        load_rows(g_raw, gout)
        q_mx = quantize("q", q_grouped)
        val_scale_pool = tile("val_scale_pool", [P, T], U8, tag="q_grouped")
        load_scale_rows(val_scale_pool, vals_scales)
        round_and_interleave(nq2_grouped, q2_raw, -1.0)
        nq2_mx = quantize("nq2", nq2_grouped)
        val_pool = tile("val_pool", [P, T], U32, tag="nq2_grouped")
        load_words(val_pool, vals_words)
        key_scales = tile("key_scales", [P, SLOTS], U8)
        nc.vector.tensor_copy(key_scales[:], key_scale_pool[:].indirect(offsets[:]))
        round_and_interleave(g_grouped, g_raw, 1.0)

        key_codes = []
        for h in range(2):
            codes = tile("key_codes%d" % h, [P, HALF], U32)
            nc.vector.tensor_copy(codes[:], key_pool[:].indirect(list_half(h)))
            key_codes.append(codes)
        old_sb = tile("old_sb", [P, T], F32, tag="warm")
        nc.sync.dma_start(out=old_sb[:], in_=old)

        a_ps = ps.tile([P, SLOTS], F32, name="a_ps")
        nb_ps = ps.tile([P, QUARTER], F32, name="nb_ps")
        dl_second = ps.tile([P, QUARTER], F32, name="dl_second")
        dl_upper = ps.tile([P, HALF], F32, name="dl_upper")
        c_ps = ps.tile([P, SLOTS], F32, name="c_ps")
        product(nb_ps[:], nq2_mx, key_codes[0][:, first], key_scales[:, first], True, True)
        product(a_ps[:, first], q_mx, key_codes[0][:, first], key_scales[:, first], True, True)
        product(dl_second[:], q_mx, key_codes[0][:, second], key_scales[:, second], True, False)
        product(dl_second[:], nq2_mx, key_codes[0][:, second], key_scales[:, second], False, True)
        product(dl_upper[:], nq2_mx, key_codes[1][:], key_scales[:, upper], True, False)
        product(dl_upper[:], q_mx, key_codes[1][:], key_scales[:, upper], False, True)

        nb = tile("nb", [P, QUARTER], F32)
        dl_first = tile("dl_first", [P, QUARTER], F32)
        nc.scalar.copy(nb[:], nb_ps[:])
        nc.vector.tensor_tensor(dl_first[:], a_ps[:, first], nb[:], ALU.add)
        product(a_ps[:, second], q_mx, key_codes[0][:, second], key_scales[:, second], True, True)
        product(a_ps[:, upper], q_mx, key_codes[1][:], key_scales[:, upper], True, True)

        sq = tile("sq", [P, SLOTS], F32)
        logden = tile("logden", [P, SLOTS], F32)
        for cols, dl in ((second, dl_second), (first, dl_first), (upper, dl_upper)):
            nc.scalar.activation(out=sq[:, cols], in_=dl[:], func=ACT.Square)
        nc.scalar.activation(out=logden[:], in_=sq[:], func=ACT.Ln, scale=sharp_col[:], bias=1.0)

        val_scales = tile("val_scales", [P, SLOTS], U8, tag="nb")
        nc.vector.tensor_copy(val_scales[:], val_scale_pool[:].indirect(offsets[:]))
        g_mx = quantize("g", g_grouped)

        neg_half_a = tile("neg_half_a", [P, SLOTS], F32, tag="q_grouped")
        neg_max = tile("neg_max", [P, 1], F32)
        nc.vector.tensor_scalar(neg_half_a[:], a_ps[:], -0.5, None, ALU.mult, ALU.min, accum_out=neg_max[:])

        val_codes = tile("val_codes", [P, SLOTS], U32)
        nc.vector.tensor_copy(val_codes[:], val_pool[:].indirect(offsets[:]))
        product(c_ps[:], g_mx, val_codes[:], val_scales[:], True, True)

        behind_vals = tile("behind_vals", [P, 2 * SLOTS + PAD], F32, tag="nq2_grouped")
        neg_logp = behind_vals[:, :SLOTS]
        pull = behind_vals[:, SLOTS : 2 * SLOTS]
        rz = behind_vals[:, 2 * SLOTS : 2 * SLOTS + 1]
        nc.vector.tensor_tensor(neg_logp, neg_half_a[:], logden[:], ALU.add)

        r = tile("r", [P, SLOTS], F32, tag="sq")
        for cols in (upper, lower):
            nc.scalar.activation(out=r[:, cols], in_=logden[:, cols], func=ACT.Exp, scale=-1.0)
        p = tile("p", [P, SLOTS], F32)
        z = tile("z", [P, 1], F32)
        nc.scalar.activation(out=p[:], in_=neg_logp, func=ACT.Exp, scale=-1.0, bias=neg_max[:], accum_out=z[:])
        for cols, dl in ((upper, dl_upper), (first, dl_first), (second, dl_second)):
            nc.vector.scalar_tensor_tensor(pull[:, cols], dl[:], sharp_col[:], r[:, cols], ALU.mult, ALU.mult)

        neg_cp = tile("neg_cp", [P, SLOTS], F32)
        neg_s = tile("neg_s", [P, 1], F32)
        nc.vector.scalar_tensor_tensor(neg_cp[:], c_ps[:], -1.0, p[:], ALU.mult, ALU.mult, accum_out=neg_s[:])

        centred = tile("centred", [P, SLOTS], F32)
        slope = tile("slope", [P, SLOTS], F32)
        for cols in (lower, upper):
            nc.scalar.activation(
                out=centred[:, cols], in_=c_ps[:, cols], func=ACT.Identity, scale=z[:], bias=neg_s[:]
            )
        for cols in (lower, upper):
            nc.vector.scalar_tensor_tensor(slope[:, cols], pull[:, cols], -0.25, p[:, cols], ALU.add, ALU.mult)
        nc.vector.reciprocal(rz, z[:])
        gain = tile("gain", [P, 1], F32)
        row_factor = tile("row_factor", [P, 1], F32)
        nc.scalar.activation(out=gain[:], in_=rz, func=ACT.Copy, scale=-1024.0)
        nc.scalar.activation(out=row_factor[:], in_=gain[:], func=ACT.Copy, scale=rz)
        for h, cols in enumerate((lower, upper)):
            nc.vector.tensor_tensor(window[:].indirect(list_half(h)), slope[:, cols], centred[:, cols], ALU.mult)

        for n in range(T // CHUNK):
            cols = slice(n * CHUNK, (n + 1) * CHUNK)
            res = tile("res%d" % n, [P, CHUNK], F32)
            nc.vector.scalar_tensor_tensor(
                res[:], window[:, cols], row_factor[:], old_sb[:, cols], ALU.mult, ALU.add
            )
            nc.sync.dma_start(out=out[:, cols], in_=res[:])
